import numpy as np
import ml_dtypes


def mxq(x, axis, fmt="e4m3"):
    dtype, down = {"e4m3": (ml_dtypes.float8_e4m3fn, 7), "e5m2": (ml_dtypes.float8_e5m2, 14)}[fmt]
    v = np.moveaxis(np.asarray(x, np.float32).astype(ml_dtypes.bfloat16).astype(np.float64), axis, -1)
    blocks = v.reshape(v.shape[:-1] + (-1, 32))
    amax = np.abs(blocks).max(-1, keepdims=True)
    byte = np.maximum(np.where(amax > 0, np.frexp(amax)[1] - 1 + 127, 0) - down, 1)
    scale = np.exp2(byte - 127.0)
    codes = (blocks / scale).astype(np.float32).astype(dtype).astype(np.float64)
    return np.moveaxis((codes * scale).reshape(v.shape), -1, axis)


WIDE = False


def mx_kscale(k):
    if not WIDE:
        return np.ones(k)
    levels = np.array([24, -24, 12, -12, 0])
    if k % 512:
        return np.exp2(np.random.permutation(np.resize(levels, k // 32))).repeat(32)
    a = np.empty((k // 512, 16))
    for p in range(k // 512):
        a[p, :8] = np.random.permutation(np.resize(levels, 8))
        for g in range(8):
            far = levels[np.abs(levels - a[p, g]) >= 10]
            a[p, g + 8] = far[np.random.randint(len(far))]
    return np.exp2(a.ravel()).repeat(32)


def f64(x):
    return np.asarray(x).astype(np.float64)


E2M1 = np.array([0.0, 0.5, 1.0, 1.5, 2.0, 3.0, 4.0, 6.0, -0.0, -0.5, -1.0, -1.5, -2.0, -3.0, -4.0, -6.0])


def pack_weight(w, fmt):
    k, n = w.shape
    w = f64(np.asarray(w, np.float32).astype(ml_dtypes.bfloat16)).reshape(k // 32, 32, n)
    amax = np.abs(w).max(1)
    if fmt == "e4m3":
        byte = np.frexp(amax)[1] - 1 + 127 - 7
    else:
        mant, ex = np.frexp(amax / 6.0)
        byte = np.where(mant > 0.5, ex, ex - 1) + 127
    byte = np.clip(np.where(amax > 0, byte, 1), 1, 254)
    scaled = (w * np.exp2(127.0 - byte)[:, None, :]).reshape(k, n).astype(np.float32)
    by_word = np.ascontiguousarray(scaled.reshape(k // 512, 128, 4, n).transpose(0, 1, 3, 2))
    if fmt == "e4m3":
        words = by_word.astype(ml_dtypes.float8_e4m3fn).view(np.uint8)
    else:
        c = by_word.astype(ml_dtypes.float4_e2m1fn).view(np.uint8) & 0xF
        words = (c[..., 0::2] | (c[..., 1::2] << 4)).reshape(k // 512, 128, 2 * n)
    return np.ascontiguousarray(words), np.ascontiguousarray(byte.astype(np.uint8).reshape(k // 512, 16, n))


def unpack_weight(words, scales, fmt):
    g, _, n = scales.shape
    words = np.ascontiguousarray(words).reshape(g, 128, n, -1)
    if fmt == "e4m3":
        vals = words.view(ml_dtypes.float8_e4m3fn).astype(np.float64)
    else:
        nib = np.empty((g, 128, n, 4), np.uint8)
        nib[..., 0::2] = words & 0xF
        nib[..., 1::2] = words >> 4
        vals = E2M1[nib]
    vals = vals * np.repeat(np.exp2(scales.astype(np.float64) - 127.0), 8, axis=1)[..., None]
    return vals.transpose(0, 1, 3, 2).reshape(g * 512, n)


def planes(y):
    n, m = y.shape
    v = y.astype(np.float32).astype(ml_dtypes.bfloat16).astype(np.float64).reshape(n // 32, 32, m)
    top = np.abs(v).max(1)
    byte = np.clip(np.where(top > 0, np.frexp(top)[1] - 1 + 127 - 7, 1), 1, 254)
    codes = (v * np.exp2(127.0 - byte)[:, None, :]).reshape(n, m).astype(np.float32).astype(ml_dtypes.float8_e4m3fn).view(np.uint8)
    words = codes.reshape(n // 512, 128, 4, m).transpose(0, 1, 3, 2)
    return np.ascontiguousarray(words), np.ascontiguousarray(byte.astype(np.uint8).reshape(n // 512, 16, m))


K, R, N, T = 1536, 1536, 512, 1536


def setup_inputs():
    n = np.random.standard_normal
    u = mx_kscale(R)[:, None]
    s = mx_kscale(K)[:, None]
    p_v4 = pack_weight(n((R, N)) / np.sqrt(R) / u, "e2m1")
    return {
        "x": (n((K, T)) * s).astype(np.float32),
        "w": (n((K, R)) / np.sqrt(K) / s).astype(np.float32),
        "sm": (np.random.uniform(0.5, 2.0, R) * u[:, 0]).astype(np.float32),
        "v4_words": p_v4[0],
        "v4_scales": p_v4[1],
        "b": (0.3 * n(N)).astype(np.float32),
    }


def reference(x, w, sm, v4_words, v4_scales, b):
    x_ = mxq(f64(x), 0, "e4m3")
    w_ = mxq(f64(w), 0, "e4m3")
    a = w_.T @ x_
    h = f64(sm)[:, None] * (np.maximum(a, 0.0)) ** 2
    h_ = mxq(h, 0, "e4m3")
    v4_ = unpack_weight(v4_words, v4_scales, "e2m1")
    y = v4_.T @ h_
    return (y + f64(b)[:, None], h) + planes(h)

@@ -1,0 +1,298 @@
+from contextlib import ExitStack
+
+import concourse.mybir as mybir
+
+K, R, N, T = 1536, 1536, 512, 1536
+FLOPS = 2 * K * R * T + 2 * R * N * T
+
+F32 = mybir.dt.float32
+BF16 = mybir.dt.bfloat16
+I32 = mybir.dt.int32
+U32 = mybir.dt.uint32
+U8 = mybir.dt.uint8
+FP8X4 = mybir.dt.float8_e4m3fn_x4
+FP4X4 = mybir.dt.float4_e2m1fn_x4
+ALU = mybir.AluOpType
+ACT = mybir.ActivationFunctionType
+
+P = 128
+PACK = 4
+BLK = 512
+NB = 3
+RAW_BUFS = 7
+
+
+def tile_mix_save_relu2_bias_kernel(tc, x, w, sm, v4_words, v4_scales, b, out_0, out_1, out_2, out_3):
+    nc = tc.nc
+    with ExitStack() as ctx:
+        keep = ctx.enter_context(tc.tile_pool(name="keep", bufs=1))
+        rawp = ctx.enter_context(tc.tile_pool(name="rawp", bufs=RAW_BUFS))
+        stage = ctx.enter_context(tc.tile_pool(name="stage", bufs=4))
+        psum = ctx.enter_context(tc.psum_pool(name="psum", bufs=8))
+        ctx.enter_context(tc.manual_schedule())
+
+        chunks = []
+        for g in range(NB):
+            chunks.extend([("w", 0, g), ("x", 0, g)])
+        for kind, blk in (("x", 1), ("w", 1), ("w", 2), ("x", 2)):
+            chunks.extend([(kind, blk, g) for g in range(NB)])
+
+        codes, scales = {}, {}
+        for key in chunks:
+            codes[key] = keep.tile([P, BLK], U32, name="c%s%d%d" % key, align_bytes=64)
+            scales[key] = keep.tile([P, BLK], U8, name="s%s%d%d" % key, align_bytes=64)
+        code_tile, h_codes, h_scales = {}, {}, {}
+        scale_tile = {}
+        for t0, t1 in ((0, 2), (2, 3)):
+            scale_tile[t1 - 1] = (keep.tile([P, NB, (t1 - t0) * BLK], U8, name="hs%d" % t0, align_bytes=64), t0 * BLK, t1 * BLK)
+            for a in range(NB):
+                tl = keep.tile([P, (t1 - t0) * BLK], U32, name="hc%d%d" % (a, t0), align_bytes=64)
+                code_tile[(a, t1 - 1)] = (tl, t0 * BLK, t1 * BLK)
+                for tb in range(t0, t1):
+                    cols = slice((tb - t0) * BLK, (tb - t0 + 1) * BLK)
+                    h_codes[(a, tb)] = tl[:, cols]
+                    h_scales[(a, tb)] = scale_tile[t1 - 1][0][:, a, cols]
+        groups = {0: [[0, 1], [2]], 1: [[0, 1], [2]], 2: [[0], [1], [2]]}
+        h_tile, h_view = {}, {}
+        for a in range(NB):
+            for grp_t in groups[a]:
+                tl = keep.tile([P, PACK, BLK * len(grp_t)], F32, name="h%d%d" % (a, grp_t[0]))
+                h_tile[(a, grp_t[-1])] = (tl, grp_t[0] * BLK, (grp_t[-1] + 1) * BLK)
+                for i, tb in enumerate(grp_t):
+                    h_view[(a, tb)] = tl[:, :, i * BLK : (i + 1) * BLK]
+        v_words = keep.tile([P, NB, 2 * N], U8, align_bytes=64)
+        v_scales = keep.tile([P, NB, N], U8, align_bytes=64)
+        sm_sb = keep.tile([P, NB, 8], F32)
+        b_sb = keep.tile([P, N // P, 8], F32)
+
+        raw, grouped, acc, relu = {}, {}, {}, {}
+
+        def load(n):
+            kind, blk, g = chunks[n]
+            src = (w if kind == "w" else x)[g * BLK : (g + 1) * BLK, blk * BLK : (blk + 1) * BLK]
+            raw[n] = rawp.tile([P, PACK, BLK], F32, name="raw")
+            nc.sync.dma_start(out=raw[n][:], in_=src.rearrange("(p j) c -> p j c", j=PACK))
+
+        def copy_on(engine, out, in_):
+            if engine == "v":
+                nc.vector.tensor_copy(out=out, in_=in_)
+            else:
+                nc.scalar.copy(out=out, in_=in_)
+
+        def interleave(engine, dst, src, c0, c1):
+            copy_on(
+                engine,
+                dst[:].rearrange("p (c i j) -> p c j i", i=4, j=PACK)[:, c0:c1],
+                src.rearrange("p j (c i) -> p c j i", i=4)[:, c0:c1],
+            )
+
+        def round_chunk(engine, n):
+            grouped[n] = stage.tile([P, PACK * BLK], BF16, name="grouped", align_bytes=64)
+            if chunks[n][0] == "x":
+                interleave(engine, grouped[n], raw[n][:], 0, BLK // 4)
+            else:
+                copy_on(
+                    engine,
+                    grouped[n][:].rearrange("p (t m j) -> p m j t", t=PACK, j=PACK),
+                    raw[n][:].rearrange("p j (m t) -> p m j t", t=PACK),
+                )
+            if n + RAW_BUFS < len(chunks):
+                load(n + RAW_BUFS)
+
+        def quantise_chunk(n):
+            key = chunks[n]
+            nc.vector.quantize_mx(out=codes[key][:].bitcast(FP8X4), scales=scales[key][:], in_=grouped[n][:])
+
+        def new_grouped(unit):
+            grouped[unit] = stage.tile([P, PACK * BLK], BF16, name="grouped", align_bytes=64)
+
+        def round_h(engine, unit, c0, c1):
+            interleave(engine, grouped[unit], h_view[unit], c0, c1)
+
+        def quantise_h(unit):
+            nc.vector.quantize_mx(out=h_codes[unit].bitcast(FP8X4), scales=h_scales[unit], in_=grouped[unit][:])
+            if unit in code_tile:
+                tl, t0, t1 = code_tile[unit]
+                nc.sync.dma_start(out=out_2[unit[0], :, t0:t1, :].rearrange("p t i -> p (t i)").bitcast(I32), in_=tl[:].bitcast(I32))
+                if unit[0] == NB - 1:
+                    tl, t0, t1 = scale_tile[unit[1]]
+                    for q in range(4):
+                        nc.sync.dma_start(
+                            out=out_3[:, 4 * q : 4 * q + 4, t0:t1].rearrange("a r t -> r a t").bitcast(I32),
+                            in_=tl[32 * q : 32 * q + 4].bitcast(I32),
+                        )
+
+        def open_banks(unit):
+            for j in range(PACK):
+                acc[(unit, j)] = psum.tile([P, BLK], F32, name="acc")
+
+        def pass_h(unit, j, g, start, stop):
+            a, tb = unit
+            cols = slice(j * P, (j + 1) * P)
+            nc.tensor.matmul_mx(
+                out=acc[(unit, j)][:],
+                lhsT=codes[("w", a, g)][:, cols].bitcast(FP8X4),
+                lhsT_scale=scales[("w", a, g)][:, cols],
+                rhs=codes[("x", tb, g)][:].bitcast(FP8X4),
+                rhs_scale=scales[("x", tb, g)][:],
+                start=start,
+                stop=stop,
+            )
+
+        def fill_h(unit):
+            open_banks(unit)
+            for j in range(PACK):
+                for g in range(NB):
+                    pass_h(unit, j, g, g == 0, g == NB - 1)
+
+        def pass_y(unit, nt, a):
+            nc.tensor.matmul_mx(
+                out=acc[(unit, nt)][:],
+                lhsT=v_words[:, a, 2 * P * nt : 2 * P * (nt + 1)].bitcast(FP4X4),
+                lhsT_scale=v_scales[:, a, P * nt : P * (nt + 1)],
+                rhs=h_codes[(a, unit[1])].bitcast(FP8X4),
+                rhs_scale=h_scales[(a, unit[1])],
+                start=(a == 0),
+                stop=(a == NB - 1),
+            )
+
+        def fill(unit):
+            if unit[0] != "y":
+                fill_h(unit)
+            else:
+                open_banks(unit)
+                for nt in range(N // P):
+                    for a in range(NB):
+                        pass_y(unit, nt, a)
+
+        def take_relu(unit, j):
+            relu[(unit, j)] = stage.tile([P, BLK], F32, name="relu")
+            nc.scalar.activation(out=relu[(unit, j)][:], in_=acc[(unit, j)][:], func=ACT.Relu)
+
+        def square(unit, j):
+            r = relu[(unit, j)]
+            nc.vector.scalar_tensor_tensor(
+                out=h_view[unit][:, j, :], in0=r[:], scalar=sm_sb[:, unit[0], j : j + 1], in1=r[:], op0=ALU.mult, op1=ALU.mult
+            )
+
+        def store_h(unit):
+            if unit in h_tile:
+                tl, t0, t1 = h_tile[unit]
+                rows = out_1[unit[0] * BLK : (unit[0] + 1) * BLK, t0:t1]
+                nc.sync.dma_start(out=rows.rearrange("(p j) t -> p j t", j=PACK), in_=tl[:])
+
+        y_tile = {}
+
+        def take_y(unit, nt):
+            if nt == 0:
+                y_tile[unit] = rawp.tile([P, N // P, BLK], F32, name="raw")
+            y = y_tile[unit]
+            if nt % 2 == 0:
+                nc.scalar.activation(out=y[:, nt, :], in_=acc[(unit, nt)][:], func=ACT.Identity, bias=b_sb[:, nt, 0:1])
+            else:
+                nc.vector.tensor_scalar(out=y[:, nt, :], in0=acc[(unit, nt)][:], scalar1=b_sb[:, nt, 0:1], scalar2=None, op0=ALU.add)
+
+        def store_y(unit, n0, n1):
+            dst = out_0[:, unit[1] * BLK : (unit[1] + 1) * BLK].rearrange("(n p) t -> p n t", p=P)
+            nc.sync.dma_start(out=dst[:, n0:n1, :], in_=y_tile[unit][:, n0:n1, :])
+
+        for n in range(4):
+            load(n)
+        nc.sync.dma_start(out=sm_sb[:, :, 0:PACK], in_=sm.rearrange("(a p j) -> p a j", p=P, j=PACK))
+        for n in range(4, RAW_BUFS):
+            load(n)
+        nc.vector.memset(v_scales[:].bitcast(I32), 0)
+
+        first = (0, 0)
+        open_banks(first)
+        for g in range(NB):
+            round_chunk("s", 2 * g)
+            round_chunk("v", 2 * g + 1)
+            quantise_chunk(2 * g)
+            quantise_chunk(2 * g + 1)
+            for j in range(PACK):
+                pass_h(first, j, g, g == 0, g == NB - 1)
+
+        order = [(0, 0), (0, 1), (1, 0), (1, 1), (2, 0), (2, 1), (0, 2), ("y", 0), (1, 2), (2, 2), ("y", 1), ("y", 2)]
+        for cyc in range(4):
+            drain, nxt = order[cyc], order[cyc + 1]
+            n0 = 6 + 3 * cyc
+            if cyc >= 2:
+                fill(nxt)
+            round_chunk("v", n0)
+            if cyc > 0:
+                quantise_h(order[cyc - 1])
+            take_relu(drain, 0)
+            square(drain, 0)
+            quantise_chunk(n0)
+            for j in range(1, PACK):
+                take_relu(drain, j)
+                square(drain, j)
+            round_chunk("s", n0 + 1)
+            if cyc == 1:
+                nc.sync.dma_start(out=v_words[:].bitcast(I32), in_=v4_words.rearrange("a p n -> p a n").bitcast(I32))
+                with nc.allow_non_contiguous_dma(reason="one bias value to a partition"):
+                    nc.sync.dma_start(out=b_sb[:, :, 0:1], in_=b.rearrange("(n p o) -> p n o", p=P, o=1))
+                for q in range(4):
+                    nc.sync.dma_start(
+                        out=v_scales[32 * q : 32 * q + 4].bitcast(I32),
+                        in_=v4_scales[:, 4 * q : 4 * q + 4, :].rearrange("a r n -> r a n").bitcast(I32),
+                    )
+            store_h(drain)
+            new_grouped(drain)
+            round_h("s", drain, 0, BLK // 4)
+            round_chunk("v", n0 + 2)
+            quantise_chunk(n0 + 1)
+            quantise_chunk(n0 + 2)
+            if cyc < 2:
+                open_banks(nxt)
+                for j in range(PACK):
+                    pass_h(nxt, j, 0, True, False)
+                for j in range(PACK):
+                    pass_h(nxt, j, 1, False, False)
+                    pass_h(nxt, j, 2, False, True)
+
+        half = BLK // 8
+        for cyc in range(4, len(order) - 1):
+            drain, before, nxt = order[cyc], order[cyc - 1], order[cyc + 1]
+            last = cyc == len(order) - 2
+            to_round = before[0] != "y" and cyc > 4
+            if last:
+                open_banks(nxt)
+                for nt in range(N // P):
+                    for a in range(NB - 1):
+                        pass_y(nxt, nt, a)
+            else:
+                fill(nxt)
+            if to_round:
+                new_grouped(before)
+            if drain[0] == "y":
+                round_h("v", before, 0, half)
+                round_h("s", before, half, 2 * half)
+                take_y(drain, 0)
+                take_y(drain, 1)
+                take_y(drain, 2)
+                quantise_h(before)
+                take_y(drain, 3)
+                store_y(drain, 0, 4)
+            else:
+                take_relu(drain, 0)
+                square(drain, 0)
+                if to_round:
+                    round_h("v", before, 0, half)
+                take_relu(drain, 1)
+                square(drain, 1)
+                if to_round:
+                    round_h("s", before, half, 2 * half)
+                if before[0] != "y":
+                    quantise_h(before)
+                for j in range(2, PACK):
+                    take_relu(drain, j)
+                    square(drain, j)
+                store_h(drain)
+        for nt in range(N // P):
+            pass_y(order[-1], nt, NB - 1)
+        for nt in range(N // P):
+            take_y(order[-1], nt)
+            if nt % 2 == 1:
+                store_y(order[-1], nt - 1, nt + 1)

@@ -1,6 +1,7 @@
 from contextlib import ExitStack
 
 import concourse.mybir as mybir
+from concourse.masks import make_identity
 
 K, R, N, T = 1536, 1536, 512, 1536
 FLOPS = 2 * K * R * T + 2 * R * N * T
@@ -19,59 +20,72 @@ P = 128
 PACK = 4
 BLK = 512
 NB = 3
-RAW_BUFS = 7
+NT = N // P
+NARROW_BUFS = 9
+QUAD = 32
 
 
 def tile_mix_save_relu2_bias_kernel(tc, x, w, sm, v4_words, v4_scales, b, out_0, out_1, out_2, out_3):
     nc = tc.nc
     with ExitStack() as ctx:
         keep = ctx.enter_context(tc.tile_pool(name="keep", bufs=1))
-        rawp = ctx.enter_context(tc.tile_pool(name="rawp", bufs=RAW_BUFS))
+        wide = ctx.enter_context(tc.tile_pool(name="wide", bufs=NB))
+        narrow = ctx.enter_context(tc.tile_pool(name="narrow", bufs=NARROW_BUFS))
         stage = ctx.enter_context(tc.tile_pool(name="stage", bufs=4))
         psum = ctx.enter_context(tc.psum_pool(name="psum", bufs=8))
         ctx.enter_context(tc.manual_schedule())
 
-        chunks = []
-        for g in range(NB):
-            chunks.extend([("w", 0, g), ("x", 0, g)])
-        for kind, blk in (("x", 1), ("w", 1), ("w", 2), ("x", 2)):
-            chunks.extend([(kind, blk, g) for g in range(NB)])
-
         codes, scales = {}, {}
-        for key in chunks:
-            codes[key] = keep.tile([P, BLK], U32, name="c%s%d%d" % key, align_bytes=64)
-            scales[key] = keep.tile([P, BLK], U8, name="s%s%d%d" % key, align_bytes=64)
-        code_tile, h_codes, h_scales = {}, {}, {}
-        scale_tile = {}
-        for t0, t1 in ((0, 2), (2, 3)):
-            scale_tile[t1 - 1] = (keep.tile([P, NB, (t1 - t0) * BLK], U8, name="hs%d" % t0, align_bytes=64), t0 * BLK, t1 * BLK)
+        for kind in ("w", "x"):
+            for blk in range(NB):
+                for g in range(NB):
+                    key = (kind, blk, g)
+                    codes[key] = keep.tile([P, BLK], U32, name="c%s%d%d" % key, align_bytes=64)
+                    scales[key] = keep.tile([P, BLK], U8, name="s%s%d%d" % key, align_bytes=64)
+        spans = ((0, 2), (2, 3))
+        code_tile, scale_tile, h_codes, h_scales = {}, {}, {}, {}
+        for t0, t1 in spans:
+            scale_tile[t1 - 1] = keep.tile([P, NB, (t1 - t0) * BLK], U8, name="hs%d" % t0, align_bytes=64)
             for a in range(NB):
-                tl = keep.tile([P, (t1 - t0) * BLK], U32, name="hc%d%d" % (a, t0), align_bytes=64)
-                code_tile[(a, t1 - 1)] = (tl, t0 * BLK, t1 * BLK)
+                code_tile[(a, t1 - 1)] = keep.tile([P, (t1 - t0) * BLK], U32, name="hc%d%d" % (a, t0), align_bytes=64)
                 for tb in range(t0, t1):
                     cols = slice((tb - t0) * BLK, (tb - t0 + 1) * BLK)
-                    h_codes[(a, tb)] = tl[:, cols]
-                    h_scales[(a, tb)] = scale_tile[t1 - 1][0][:, a, cols]
-        groups = {0: [[0, 1], [2]], 1: [[0, 1], [2]], 2: [[0], [1], [2]]}
-        h_tile, h_view = {}, {}
-        for a in range(NB):
-            for grp_t in groups[a]:
-                tl = keep.tile([P, PACK, BLK * len(grp_t)], F32, name="h%d%d" % (a, grp_t[0]))
-                h_tile[(a, grp_t[-1])] = (tl, grp_t[0] * BLK, (grp_t[-1] + 1) * BLK)
-                for i, tb in enumerate(grp_t):
-                    h_view[(a, tb)] = tl[:, :, i * BLK : (i + 1) * BLK]
+                    h_codes[(a, tb)] = code_tile[(a, t1 - 1)][:, cols]
+                    h_scales[(a, tb)] = scale_tile[t1 - 1][:, a, cols]
+        span_cols = {t1 - 1: slice(t0 * BLK, t1 * BLK) for t0, t1 in spans}
         v_words = keep.tile([P, NB, 2 * N], U8, align_bytes=64)
         v_scales = keep.tile([P, NB, N], U8, align_bytes=64)
-        sm_sb = keep.tile([P, NB, 8], F32)
-        b_sb = keep.tile([P, N // P, 8], F32)
+        sm_rows = keep.tile([P, BLK], F32)
+        b_rows = keep.tile([P, P], F32)
+        ident = keep.tile([P, P], F32)
+        sm_sb = keep.tile([P, PACK, NB], F32)
+        b_sb = keep.tile([P, NT], F32)
 
-        raw, grouped, acc, relu = {}, {}, {}, {}
+        raw, grouped, acc, issued, res_tile, res_view = {}, {}, {}, {}, {}, {}
+        done = set()
+        order = [(0, 0), (0, 1), (1, 0), (1, 1), (2, 0), (2, 1), (0, 2), ("y", 0), ("y", 1), (1, 2), (2, 2), ("y", 2)]
 
-        def load(n):
-            kind, blk, g = chunks[n]
-            src = (w if kind == "w" else x)[g * BLK : (g + 1) * BLK, blk * BLK : (blk + 1) * BLK]
-            raw[n] = rawp.tile([P, PACK, BLK], F32, name="raw")
-            nc.sync.dma_start(out=raw[n][:], in_=src.rearrange("(p j) c -> p j c", j=PACK))
+        def load(kind, b0, b1, g):
+            src = (w if kind == "w" else x)[g * BLK : (g + 1) * BLK, b0 * BLK : b1 * BLK]
+            if b1 - b0 == 2:
+                tl = wide.tile([P, PACK, 2 * BLK], F32, name="wide")
+            else:
+                tl = narrow.tile([P, PACK, BLK], F32, name="narrow")
+            nc.sync.dma_start(out=tl[:], in_=src.rearrange("(p j) c -> p j c", j=PACK))
+            for blk in range(b0, b1):
+                raw[(kind, blk, g)] = tl[:, :, (blk - b0) * BLK : (blk - b0 + 1) * BLK]
+
+        def result_tile(unit):
+            row, tb = unit
+            if tb == 0:
+                tl = wide.tile([P, PACK, 2 * BLK], F32, name="wide")
+                res_tile[(row, 1)] = tl
+                res_view[(row, 0)] = tl[:, :, 0:BLK]
+                res_view[(row, 1)] = tl[:, :, BLK : 2 * BLK]
+            if tb == 2:
+                tl = narrow.tile([P, PACK, BLK], F32, name="narrow")
+                res_tile[unit] = tl
+                res_view[unit] = tl[:]
 
         def copy_on(engine, out, in_):
             if engine == "v":
@@ -79,220 +93,203 @@ def tile_mix_save_relu2_bias_kernel(tc, x, w, sm, v4_words, v4_scales, b, out_0,
             else:
                 nc.scalar.copy(out=out, in_=in_)
 
-        def interleave(engine, dst, src, c0, c1):
+        def new_grouped(key):
+            grouped[key] = stage.tile([P, PACK * BLK], BF16, name="grouped", align_bytes=64)
+
+        def interleave(engine, key, src, c0, c1):
             copy_on(
                 engine,
-                dst[:].rearrange("p (c i j) -> p c j i", i=4, j=PACK)[:, c0:c1],
+                grouped[key][:].rearrange("p (c i j) -> p c j i", i=4, j=PACK)[:, c0:c1],
                 src.rearrange("p j (c i) -> p c j i", i=4)[:, c0:c1],
             )
 
-        def round_chunk(engine, n):
-            grouped[n] = stage.tile([P, PACK * BLK], BF16, name="grouped", align_bytes=64)
-            if chunks[n][0] == "x":
-                interleave(engine, grouped[n], raw[n][:], 0, BLK // 4)
+        def round_chunk(engine, key):
+            new_grouped(key)
+            if key[0] == "x":
+                interleave(engine, key, raw[key], 0, BLK // 4)
             else:
                 copy_on(
                     engine,
-                    grouped[n][:].rearrange("p (t m j) -> p m j t", t=PACK, j=PACK),
-                    raw[n][:].rearrange("p j (m t) -> p m j t", t=PACK),
+                    grouped[key][:].rearrange("p (t m j) -> p m j t", t=PACK, j=PACK),
+                    raw[key].rearrange("p j (m t) -> p m j t", t=PACK),
                 )
-            if n + RAW_BUFS < len(chunks):
-                load(n + RAW_BUFS)
 
-        def quantise_chunk(n):
-            key = chunks[n]
-            nc.vector.quantize_mx(out=codes[key][:].bitcast(FP8X4), scales=scales[key][:], in_=grouped[n][:])
-
-        def new_grouped(unit):
-            grouped[unit] = stage.tile([P, PACK * BLK], BF16, name="grouped", align_bytes=64)
+        def quantise_chunk(key):
+            nc.vector.quantize_mx(out=codes[key][:].bitcast(FP8X4), scales=scales[key][:], in_=grouped[key][:])
+            done.add(key)
 
         def round_h(engine, unit, c0, c1):
-            interleave(engine, grouped[unit], h_view[unit], c0, c1)
+            interleave(engine, unit, res_view[unit], c0, c1)
 
         def quantise_h(unit):
+            a, tb = unit
             nc.vector.quantize_mx(out=h_codes[unit].bitcast(FP8X4), scales=h_scales[unit], in_=grouped[unit][:])
-            if unit in code_tile:
-                tl, t0, t1 = code_tile[unit]
-                nc.sync.dma_start(out=out_2[unit[0], :, t0:t1, :].rearrange("p t i -> p (t i)").bitcast(I32), in_=tl[:].bitcast(I32))
-                if unit[0] == NB - 1:
-                    tl, t0, t1 = scale_tile[unit[1]]
-                    for q in range(4):
+            done.add(unit)
+            if tb in span_cols:
+                nc.sync.dma_start(
+                    out=out_2[a, :, span_cols[tb], :].rearrange("p t i -> p (t i)").bitcast(I32), in_=code_tile[unit][:].bitcast(I32)
+                )
+                if a == NB - 1:
+                    for r in range(4):
                         nc.sync.dma_start(
-                            out=out_3[:, 4 * q : 4 * q + 4, t0:t1].rearrange("a r t -> r a t").bitcast(I32),
-                            in_=tl[32 * q : 32 * q + 4].bitcast(I32),
+                            out=out_3[:, r::4, span_cols[tb]].rearrange("a q t -> q a t").bitcast(I32),
+                            in_=scale_tile[tb][r:P:QUAD].bitcast(I32),
                         )
 
         def open_banks(unit):
             for j in range(PACK):
                 acc[(unit, j)] = psum.tile([P, BLK], F32, name="acc")
 
-        def pass_h(unit, j, g, start, stop):
-            a, tb = unit
-            cols = slice(j * P, (j + 1) * P)
-            nc.tensor.matmul_mx(
-                out=acc[(unit, j)][:],
-                lhsT=codes[("w", a, g)][:, cols].bitcast(FP8X4),
-                lhsT_scale=scales[("w", a, g)][:, cols],
-                rhs=codes[("x", tb, g)][:].bitcast(FP8X4),
-                rhs_scale=scales[("x", tb, g)][:],
-                start=start,
-                stop=stop,
-            )
-
-        def fill_h(unit):
-            open_banks(unit)
-            for j in range(PACK):
-                for g in range(NB):
-                    pass_h(unit, j, g, g == 0, g == NB - 1)
-
-        def pass_y(unit, nt, a):
-            nc.tensor.matmul_mx(
-                out=acc[(unit, nt)][:],
-                lhsT=v_words[:, a, 2 * P * nt : 2 * P * (nt + 1)].bitcast(FP4X4),
-                lhsT_scale=v_scales[:, a, P * nt : P * (nt + 1)],
-                rhs=h_codes[(a, unit[1])].bitcast(FP8X4),
-                rhs_scale=h_scales[(a, unit[1])],
-                start=(a == 0),
-                stop=(a == NB - 1),
-            )
-
-        def fill(unit):
-            if unit[0] != "y":
-                fill_h(unit)
+        def one_pass(unit, j, g):
+            row, tb = unit
+            if row == "y":
+                lhs = v_words[:, g, 2 * P * j : 2 * P * (j + 1)].bitcast(FP4X4)
+                lhs_scale = v_scales[:, g, P * j : P * (j + 1)]
+                rhs, rhs_scale = h_codes[(g, tb)], h_scales[(g, tb)]
             else:
-                open_banks(unit)
-                for nt in range(N // P):
-                    for a in range(NB):
-                        pass_y(unit, nt, a)
-
-        def take_relu(unit, j):
-            relu[(unit, j)] = stage.tile([P, BLK], F32, name="relu")
-            nc.scalar.activation(out=relu[(unit, j)][:], in_=acc[(unit, j)][:], func=ACT.Relu)
-
-        def square(unit, j):
-            r = relu[(unit, j)]
-            nc.vector.scalar_tensor_tensor(
-                out=h_view[unit][:, j, :], in0=r[:], scalar=sm_sb[:, unit[0], j : j + 1], in1=r[:], op0=ALU.mult, op1=ALU.mult
+                lhs = codes[("w", row, g)][:, P * j : P * (j + 1)].bitcast(FP8X4)
+                lhs_scale = scales[("w", row, g)][:, P * j : P * (j + 1)]
+                rhs, rhs_scale = codes[("x", tb, g)][:], scales[("x", tb, g)][:]
+            nc.tensor.matmul_mx(
+                out=acc[(unit, j)][:], lhsT=lhs, lhsT_scale=lhs_scale, rhs=rhs.bitcast(FP8X4), rhs_scale=rhs_scale,
+                start=(g == 0), stop=(g == NB - 1),
             )
 
-        def store_h(unit):
-            if unit in h_tile:
-                tl, t0, t1 = h_tile[unit]
-                rows = out_1[unit[0] * BLK : (unit[0] + 1) * BLK, t0:t1]
-                nc.sync.dma_start(out=rows.rearrange("(p j) t -> p j t", j=PACK), in_=tl[:])
+        def has_operands(unit, g):
+            row, tb = unit
+            if row == "y":
+                return (g, tb) in done
+            return ("w", row, g) in done and ("x", tb, g) in done
 
-        y_tile = {}
+        def issue_passes(upto):
+            for unit in order[: upto + 1]:
+                g0 = issued.get(unit, 0)
+                ready = [g for g in range(g0, NB) if all(has_operands(unit, e) for e in range(g0, g + 1))]
+                if g0 == 0 and not ready:
+                    return
+                if g0 == 0:
+                    open_banks(unit)
+                for j in range(PACK):
+                    for g in ready:
+                        one_pass(unit, j, g)
+                issued[unit] = g0 + len(ready)
 
-        def take_y(unit, nt):
-            if nt == 0:
-                y_tile[unit] = rawp.tile([P, N // P, BLK], F32, name="raw")
-            y = y_tile[unit]
-            if nt % 2 == 0:
-                nc.scalar.activation(out=y[:, nt, :], in_=acc[(unit, nt)][:], func=ACT.Identity, bias=b_sb[:, nt, 0:1])
+        def take(unit, j):
+            row = unit[0]
+            if j == 0:
+                result_tile(unit)
+            dst = res_view[unit][:, j, :]
+            if row != "y":
+                r = stage.tile([P, BLK], F32, name="relu")
+                nc.scalar.activation(out=r[:], in_=acc[(unit, j)][:], func=ACT.Relu)
+                nc.vector.scalar_tensor_tensor(out=dst, in0=r[:], scalar=sm_sb[:, j, row : row + 1], in1=r[:], op0=ALU.mult, op1=ALU.mult)
+            elif j % 2 == 0:
+                nc.scalar.activation(out=dst, in_=acc[(unit, j)][:], func=ACT.Identity, bias=b_sb[:, j : j + 1])
             else:
-                nc.vector.tensor_scalar(out=y[:, nt, :], in0=acc[(unit, nt)][:], scalar1=b_sb[:, nt, 0:1], scalar2=None, op0=ALU.add)
+                nc.vector.tensor_scalar(out=dst, in0=acc[(unit, j)][:], scalar1=b_sb[:, j : j + 1], scalar2=None, op0=ALU.add)
 
-        def store_y(unit, n0, n1):
-            dst = out_0[:, unit[1] * BLK : (unit[1] + 1) * BLK].rearrange("(n p) t -> p n t", p=P)
-            nc.sync.dma_start(out=dst[:, n0:n1, :], in_=y_tile[unit][:, n0:n1, :])
+        def store(unit, j0, j1):
+            row, tb = unit
+            if tb in span_cols:
+                if row == "y":
+                    dst = out_0[:, span_cols[tb]].rearrange("(j p) t -> p j t", p=P)
+                else:
+                    dst = out_1[row * BLK : (row + 1) * BLK, span_cols[tb]].rearrange("(p j) t -> p j t", j=PACK)
+                nc.sync.dma_start(out=dst[:, j0:j1, :], in_=res_tile[unit][:, j0:j1, :])
 
-        for n in range(4):
-            load(n)
-        nc.sync.dma_start(out=sm_sb[:, :, 0:PACK], in_=sm.rearrange("(a p j) -> p a j", p=P, j=PACK))
-        for n in range(4, RAW_BUFS):
-            load(n)
+        nc.vector.memset(sm_rows[:], 0.0)
+        nc.vector.memset(b_rows[:], 0.0)
         nc.vector.memset(v_scales[:].bitcast(I32), 0)
-
-        first = (0, 0)
-        open_banks(first)
+        make_identity(nc, ident[:])
+        chunks = []
         for g in range(NB):
-            round_chunk("s", 2 * g)
-            round_chunk("v", 2 * g + 1)
-            quantise_chunk(2 * g)
-            quantise_chunk(2 * g + 1)
-            for j in range(PACK):
-                pass_h(first, j, g, g == 0, g == NB - 1)
+            chunks.extend([("w", 0, g), ("x", 0, g)])
+        later = [("x", 1), ("w", 1), ("w", 2), ("x", 2)]
+        for kind, blk in later:
+            chunks.extend([(kind, blk, g) for g in range(NB)])
 
-        order = [(0, 0), (0, 1), (1, 0), (1, 1), (2, 0), (2, 1), (0, 2), ("y", 0), (1, 2), (2, 2), ("y", 1), ("y", 2)]
-        for cyc in range(4):
-            drain, nxt = order[cyc], order[cyc + 1]
-            n0 = 6 + 3 * cyc
-            if cyc >= 2:
-                fill(nxt)
-            round_chunk("v", n0)
-            if cyc > 0:
-                quantise_h(order[cyc - 1])
-            take_relu(drain, 0)
-            square(drain, 0)
-            quantise_chunk(n0)
-            for j in range(1, PACK):
-                take_relu(drain, j)
-                square(drain, j)
-            round_chunk("s", n0 + 1)
-            if cyc == 1:
+        def load_chunk(n):
+            if n < len(chunks):
+                kind, blk, g = chunks[n]
+                load(kind, blk, blk + 1, g)
+            if n == len(chunks) - 1:
                 nc.sync.dma_start(out=v_words[:].bitcast(I32), in_=v4_words.rearrange("a p n -> p a n").bitcast(I32))
-                with nc.allow_non_contiguous_dma(reason="one bias value to a partition"):
-                    nc.sync.dma_start(out=b_sb[:, :, 0:1], in_=b.rearrange("(n p o) -> p n o", p=P, o=1))
-                for q in range(4):
+                for r in range(4):
                     nc.sync.dma_start(
-                        out=v_scales[32 * q : 32 * q + 4].bitcast(I32),
-                        in_=v4_scales[:, 4 * q : 4 * q + 4, :].rearrange("a r n -> r a n").bitcast(I32),
+                        out=v_scales[r:P:QUAD].bitcast(I32), in_=v4_scales[:, r::4, :].rearrange("a q n -> q a n").bitcast(I32)
                     )
-            store_h(drain)
-            new_grouped(drain)
-            round_h("s", drain, 0, BLK // 4)
-            round_chunk("v", n0 + 2)
-            quantise_chunk(n0 + 1)
-            quantise_chunk(n0 + 2)
-            if cyc < 2:
-                open_banks(nxt)
-                for j in range(PACK):
-                    pass_h(nxt, j, 0, True, False)
-                for j in range(PACK):
-                    pass_h(nxt, j, 1, False, False)
-                    pass_h(nxt, j, 2, False, True)
+
+        def prepare(engine, key):
+            round_chunk(engine, key)
+            load_chunk(chunks.index(key) + NARROW_BUFS)
+
+        load_chunk(0)
+        nc.sync.dma_start(out=sm_rows[0:NB, :], in_=sm.rearrange("(a c) -> a c", a=NB))
+        nc.sync.dma_start(out=b_rows[0:NT, :], in_=b.rearrange("(n p) -> n p", p=P))
+        for n in range(1, NARROW_BUFS):
+            load_chunk(n)
+
+        sm_t = psum.tile([P, PACK, P], F32, name="acc")
+        b_t = psum.tile([P, P], F32, name="acc")
+        for j in range(PACK):
+            nc.tensor.transpose(sm_t[:, j, :], sm_rows[:, j:BLK:PACK], ident[:])
+        nc.tensor.transpose(b_t[:], b_rows[:], ident[:])
+        nc.vector.tensor_copy(out=sm_sb[:], in_=sm_t[:, :, 0:NB])
+        nc.vector.tensor_copy(out=b_sb[:], in_=b_t[:, 0:NT])
+
+        for g in range(NB):
+            prepare("s", ("w", 0, g))
+            prepare("v", ("x", 0, g))
+            quantise_chunk(("w", 0, g))
+            quantise_chunk(("x", 0, g))
+            issue_passes(0)
 
         half = BLK // 8
-        for cyc in range(4, len(order) - 1):
-            drain, before, nxt = order[cyc], order[cyc - 1], order[cyc + 1]
-            last = cyc == len(order) - 2
-            to_round = before[0] != "y" and cyc > 4
-            if last:
-                open_banks(nxt)
-                for nt in range(N // P):
-                    for a in range(NB - 1):
-                        pass_y(nxt, nt, a)
+        rounded = set()
+        for cyc, drain in enumerate(order):
+            waiting = [u for u in order[:cyc] if u[0] != "y" and u not in done]
+            if cyc < len(later):
+                keys = [later[cyc] + (g,) for g in range(NB)]
+                prepare("v", keys[0])
+                for u in waiting:
+                    quantise_h(u)
+                take(drain, 0)
+                quantise_chunk(keys[0])
+                issue_passes(cyc + 1)
+                for j in range(1, PACK):
+                    take(drain, j)
+                prepare("s", keys[1])
+                new_grouped(drain)
+                round_h("s", drain, 0, 2 * half)
+                rounded.add(drain)
+                prepare("v", keys[2])
+                quantise_chunk(keys[1])
+                quantise_chunk(keys[2])
+                store(drain, 0, PACK)
+            elif cyc < len(order) - 1:
+                to_round = [u for u in waiting if u not in rounded]
+                for u in to_round:
+                    new_grouped(u)
+                take(drain, 0)
+                for u in to_round:
+                    round_h("v", u, 0, half)
+                take(drain, 1)
+                for u in to_round:
+                    round_h("s", u, half, 2 * half)
+                for u in waiting:
+                    quantise_h(u)
+                take(drain, 2)
+                take(drain, 3)
+                store(drain, 0, PACK)
             else:
-                fill(nxt)
-            if to_round:
-                new_grouped(before)
-            if drain[0] == "y":
-                round_h("v", before, 0, half)
-                round_h("s", before, half, 2 * half)
-                take_y(drain, 0)
-                take_y(drain, 1)
-                take_y(drain, 2)
-                quantise_h(before)
-                take_y(drain, 3)
-                store_y(drain, 0, 4)
-            else:
-                take_relu(drain, 0)
-                square(drain, 0)
-                if to_round:
-                    round_h("v", before, 0, half)
-                take_relu(drain, 1)
-                square(drain, 1)
-                if to_round:
-                    round_h("s", before, half, 2 * half)
-                if before[0] != "y":
-                    quantise_h(before)
-                for j in range(2, PACK):
-                    take_relu(drain, j)
-                    square(drain, j)
-                store_h(drain)
-        for nt in range(N // P):
-            pass_y(order[-1], nt, NB - 1)
-        for nt in range(N // P):
-            take_y(order[-1], nt)
-            if nt % 2 == 1:
-                store_y(order[-1], nt - 1, nt + 1)
+                for u in waiting:
+                    new_grouped(u)
+                    round_h("v", u, 0, half)
+                    round_h("s", u, half, 2 * half)
+                    quantise_h(u)
+                issue_passes(cyc)
+                for j in range(PACK):
+                    take(drain, j)
+                    if j % 2 == 1:
+                        store(drain, j - 1, j + 1)
+            issue_passes(cyc + 2)

@@ -23,13 +23,18 @@ NB = 3
 NT = N // P
 NARROW_BUFS = 9
 QUAD = 32
+JOINED = (0, 1)
+WHOLE = 3
+RELU_BUFS = 4
+LATE_V = 64
+LAST_V = 64
 
 
 def tile_mix_save_relu2_bias_kernel(tc, x, w, sm, v4_words, v4_scales, b, out_0, out_1, out_2, out_3):
     nc = tc.nc
     with ExitStack() as ctx:
         keep = ctx.enter_context(tc.tile_pool(name="keep", bufs=1))
-        wide = ctx.enter_context(tc.tile_pool(name="wide", bufs=NB))
+        wide = ctx.enter_context(tc.tile_pool(name="wide", bufs=2))
         narrow = ctx.enter_context(tc.tile_pool(name="narrow", bufs=NARROW_BUFS))
         stage = ctx.enter_context(tc.tile_pool(name="stage", bufs=4))
         psum = ctx.enter_context(tc.psum_pool(name="psum", bufs=8))
@@ -40,51 +45,51 @@ def tile_mix_save_relu2_bias_kernel(tc, x, w, sm, v4_words, v4_scales, b, out_0,
             for blk in range(NB):
                 for g in range(NB):
                     key = (kind, blk, g)
-                    codes[key] = keep.tile([P, BLK], U32, name="c%s%d%d" % key, align_bytes=64)
-                    scales[key] = keep.tile([P, BLK], U8, name="s%s%d%d" % key, align_bytes=64)
+                    codes[key] = keep.tile([P, BLK], U32, name="c%s%d%d" % key, align_bytes=256)
+                    scales[key] = keep.tile([P, BLK], U8, name="s%s%d%d" % key, align_bytes=256)
         spans = ((0, 2), (2, 3))
         code_tile, scale_tile, h_codes, h_scales = {}, {}, {}, {}
         for t0, t1 in spans:
-            scale_tile[t1 - 1] = keep.tile([P, NB, (t1 - t0) * BLK], U8, name="hs%d" % t0, align_bytes=64)
+            scale_tile[t1 - 1] = keep.tile([P, NB, (t1 - t0) * BLK], U8, name="hs%d" % t0, align_bytes=256)
             for a in range(NB):
-                code_tile[(a, t1 - 1)] = keep.tile([P, (t1 - t0) * BLK], U32, name="hc%d%d" % (a, t0), align_bytes=64)
+                code_tile[(a, t1 - 1)] = keep.tile([P, (t1 - t0) * BLK], U32, name="hc%d%d" % (a, t0), align_bytes=256)
                 for tb in range(t0, t1):
                     cols = slice((tb - t0) * BLK, (tb - t0 + 1) * BLK)
                     h_codes[(a, tb)] = code_tile[(a, t1 - 1)][:, cols]
                     h_scales[(a, tb)] = scale_tile[t1 - 1][:, a, cols]
         span_cols = {t1 - 1: slice(t0 * BLK, t1 * BLK) for t0, t1 in spans}
-        v_words = keep.tile([P, NB, 2 * N], U8, align_bytes=64)
-        v_scales = keep.tile([P, NB, N], U8, align_bytes=64)
-        sm_rows = keep.tile([P, BLK], F32)
-        b_rows = keep.tile([P, P], F32)
-        ident = keep.tile([P, P], F32)
+        v_words = keep.tile([P, NB, 2 * N], U8, align_bytes=256)
+        v_scales = keep.tile([P, NB, N], U8, align_bytes=256)
+        sm_rows = keep.tile([P, BLK], F32, align_bytes=256)
+        b_rows = keep.tile([P, P], F32, align_bytes=256)
+        ident = keep.tile([P, P], F32, align_bytes=256)
         sm_sb = keep.tile([P, PACK, NB], F32)
         b_sb = keep.tile([P, NT], F32)
 
         raw, grouped, acc, issued, res_tile, res_view = {}, {}, {}, {}, {}, {}
         done = set()
-        order = [(0, 0), (0, 1), (1, 0), (1, 1), (2, 0), (2, 1), (0, 2), ("y", 0), ("y", 1), (1, 2), (2, 2), ("y", 2)]
+        order = [(0, 0), (0, 1), (1, 0), (1, 1), (2, 0), (2, 1), (0, 2), (1, 2), ("y", 0), (2, 2), ("y", 1), ("y", 2)]
 
         def load(kind, b0, b1, g):
             src = (w if kind == "w" else x)[g * BLK : (g + 1) * BLK, b0 * BLK : b1 * BLK]
             if b1 - b0 == 2:
-                tl = wide.tile([P, PACK, 2 * BLK], F32, name="wide")
+                tl = wide.tile([P, PACK, 2 * BLK], F32, name="wide", align_bytes=256)
             else:
-                tl = narrow.tile([P, PACK, BLK], F32, name="narrow")
+                tl = narrow.tile([P, PACK, BLK], F32, name="narrow", align_bytes=256)
             nc.sync.dma_start(out=tl[:], in_=src.rearrange("(p j) c -> p j c", j=PACK))
             for blk in range(b0, b1):
                 raw[(kind, blk, g)] = tl[:, :, (blk - b0) * BLK : (blk - b0 + 1) * BLK]
 
         def result_tile(unit):
             row, tb = unit
-            if tb == 0:
-                tl = wide.tile([P, PACK, 2 * BLK], F32, name="wide")
-                res_tile[(row, 1)] = tl
+            if row in JOINED and tb == 0:
+                tl = wide.tile([P, PACK, 2 * BLK], F32, name="wide", align_bytes=256)
+                res_tile[(row, 1)] = (tl, slice(0, 2 * BLK))
                 res_view[(row, 0)] = tl[:, :, 0:BLK]
                 res_view[(row, 1)] = tl[:, :, BLK : 2 * BLK]
-            if tb == 2:
-                tl = narrow.tile([P, PACK, BLK], F32, name="narrow")
-                res_tile[unit] = tl
+            elif unit not in res_view:
+                tl = narrow.tile([P, PACK, BLK], F32, name="narrow", align_bytes=256)
+                res_tile[unit] = (tl, slice(tb * BLK, (tb + 1) * BLK))
                 res_view[unit] = tl[:]
 
         def copy_on(engine, out, in_):
@@ -94,7 +99,7 @@ def tile_mix_save_relu2_bias_kernel(tc, x, w, sm, v4_words, v4_scales, b, out_0,
                 nc.scalar.copy(out=out, in_=in_)
 
         def new_grouped(key):
-            grouped[key] = stage.tile([P, PACK * BLK], BF16, name="grouped", align_bytes=64)
+            grouped[key] = stage.tile([P, PACK * BLK], BF16, name="grouped", align_bytes=256)
 
         def interleave(engine, key, src, c0, c1):
             copy_on(
@@ -130,10 +135,10 @@ def tile_mix_save_relu2_bias_kernel(tc, x, w, sm, v4_words, v4_scales, b, out_0,
                     out=out_2[a, :, span_cols[tb], :].rearrange("p t i -> p (t i)").bitcast(I32), in_=code_tile[unit][:].bitcast(I32)
                 )
                 if a == NB - 1:
-                    for r in range(4):
+                    for q in (0, 2, 1, 3):
                         nc.sync.dma_start(
-                            out=out_3[:, r::4, span_cols[tb]].rearrange("a q t -> q a t").bitcast(I32),
-                            in_=scale_tile[tb][r:P:QUAD].bitcast(I32),
+                            out=out_3[:, 4 * q : 4 * q + 4, span_cols[tb]].rearrange("a r t -> r a t").bitcast(I32),
+                            in_=scale_tile[tb][QUAD * q : QUAD * q + 4].bitcast(I32),
                         )
 
         def open_banks(unit):
@@ -180,7 +185,7 @@ def tile_mix_save_relu2_bias_kernel(tc, x, w, sm, v4_words, v4_scales, b, out_0,
                 result_tile(unit)
             dst = res_view[unit][:, j, :]
             if row != "y":
-                r = stage.tile([P, BLK], F32, name="relu")
+                r = stage.tile([P, BLK], F32, name="relu", align_bytes=256, bufs=RELU_BUFS)
                 nc.scalar.activation(out=r[:], in_=acc[(unit, j)][:], func=ACT.Relu)
                 nc.vector.scalar_tensor_tensor(out=dst, in0=r[:], scalar=sm_sb[:, j, row : row + 1], in1=r[:], op0=ALU.mult, op1=ALU.mult)
             elif j % 2 == 0:
@@ -189,13 +194,14 @@ def tile_mix_save_relu2_bias_kernel(tc, x, w, sm, v4_words, v4_scales, b, out_0,
                 nc.vector.tensor_scalar(out=dst, in0=acc[(unit, j)][:], scalar1=b_sb[:, j : j + 1], scalar2=None, op0=ALU.add)
 
         def store(unit, j0, j1):
-            row, tb = unit
-            if tb in span_cols:
+            row = unit[0]
+            if unit in res_tile:
+                tl, cols = res_tile[unit]
                 if row == "y":
-                    dst = out_0[:, span_cols[tb]].rearrange("(j p) t -> p j t", p=P)
+                    dst = out_0[:, cols].rearrange("(j p) t -> p j t", p=P)
                 else:
-                    dst = out_1[row * BLK : (row + 1) * BLK, span_cols[tb]].rearrange("(p j) t -> p j t", j=PACK)
-                nc.sync.dma_start(out=dst[:, j0:j1, :], in_=res_tile[unit][:, j0:j1, :])
+                    dst = out_1[row * BLK : (row + 1) * BLK, cols].rearrange("(p j) t -> p j t", j=PACK)
+                nc.sync.dma_start(out=dst[:, j0:j1, :], in_=tl[:, j0:j1, :])
 
         nc.vector.memset(sm_rows[:], 0.0)
         nc.vector.memset(b_rows[:], 0.0)
@@ -214,9 +220,10 @@ def tile_mix_save_relu2_bias_kernel(tc, x, w, sm, v4_words, v4_scales, b, out_0,
                 load(kind, blk, blk + 1, g)
             if n == len(chunks) - 1:
                 nc.sync.dma_start(out=v_words[:].bitcast(I32), in_=v4_words.rearrange("a p n -> p a n").bitcast(I32))
-                for r in range(4):
+                for q in (0, 2, 1, 3):
                     nc.sync.dma_start(
-                        out=v_scales[r:P:QUAD].bitcast(I32), in_=v4_scales[:, r::4, :].rearrange("a q n -> q a n").bitcast(I32)
+                        out=v_scales[QUAD * q : QUAD * q + 4].bitcast(I32),
+                        in_=v4_scales[:, 4 * q : 4 * q + 4, :].rearrange("a r n -> r a n").bitcast(I32),
                     )
 
         def prepare(engine, key):
@@ -234,8 +241,6 @@ def tile_mix_save_relu2_bias_kernel(tc, x, w, sm, v4_words, v4_scales, b, out_0,
         for j in range(PACK):
             nc.tensor.transpose(sm_t[:, j, :], sm_rows[:, j:BLK:PACK], ident[:])
         nc.tensor.transpose(b_t[:], b_rows[:], ident[:])
-        nc.vector.tensor_copy(out=sm_sb[:], in_=sm_t[:, :, 0:NB])
-        nc.vector.tensor_copy(out=b_sb[:], in_=b_t[:, 0:NT])
 
         for g in range(NB):
             prepare("s", ("w", 0, g))
@@ -243,6 +248,9 @@ def tile_mix_save_relu2_bias_kernel(tc, x, w, sm, v4_words, v4_scales, b, out_0,
             quantise_chunk(("w", 0, g))
             quantise_chunk(("x", 0, g))
             issue_passes(0)
+            if g == 1:
+                nc.vector.tensor_copy(out=sm_sb[:], in_=sm_t[:, :, 0:NB])
+                nc.vector.tensor_copy(out=b_sb[:], in_=b_t[:, 0:NT])
 
         half = BLK // 8
         rounded = set()
@@ -259,23 +267,25 @@ def tile_mix_save_relu2_bias_kernel(tc, x, w, sm, v4_words, v4_scales, b, out_0,
                 for j in range(1, PACK):
                     take(drain, j)
                 prepare("s", keys[1])
-                new_grouped(drain)
-                round_h("s", drain, 0, 2 * half)
-                rounded.add(drain)
+                if cyc < WHOLE:
+                    new_grouped(drain)
+                    round_h("s", drain, 0, 2 * half)
+                    rounded.add(drain)
                 prepare("v", keys[2])
                 quantise_chunk(keys[1])
                 quantise_chunk(keys[2])
                 store(drain, 0, PACK)
             elif cyc < len(order) - 1:
                 to_round = [u for u in waiting if u not in rounded]
+                share = LAST_V if to_round == [(NB - 1, NB - 1)] else LATE_V
                 for u in to_round:
                     new_grouped(u)
                 take(drain, 0)
                 for u in to_round:
-                    round_h("v", u, 0, half)
+                    round_h("v", u, 0, share)
                 take(drain, 1)
                 for u in to_round:
-                    round_h("s", u, half, 2 * half)
+                    round_h("s", u, share, 2 * half)
                 for u in waiting:
                     quantise_h(u)
                 take(drain, 2)
@@ -284,8 +294,8 @@ def tile_mix_save_relu2_bias_kernel(tc, x, w, sm, v4_words, v4_scales, b, out_0,
             else:
                 for u in waiting:
                     new_grouped(u)
-                    round_h("v", u, 0, half)
-                    round_h("s", u, half, 2 * half)
+                    round_h("v", u, 0, LAST_V)
+                    round_h("s", u, LAST_V, 2 * half)
                     quantise_h(u)
                 issue_passes(cyc)
                 for j in range(PACK):

from contextlib import ExitStack

import concourse.mybir as mybir
from concourse.masks import make_identity

K, R, N, T = 1536, 1536, 512, 1536
FLOPS = 2 * K * R * T + 2 * R * N * T

F32 = mybir.dt.float32
BF16 = mybir.dt.bfloat16
I32 = mybir.dt.int32
U32 = mybir.dt.uint32
U8 = mybir.dt.uint8
FP8X4 = mybir.dt.float8_e4m3fn_x4
FP4X4 = mybir.dt.float4_e2m1fn_x4
ALU = mybir.AluOpType
ACT = mybir.ActivationFunctionType

P = 128
PACK = 4
BLK = 512
NB = 3
NT = N // P
NARROW_BUFS = 9
QUAD = 32
JOINED = (0, 1)
WHOLE = 3
RELU_BUFS = 4
LATE_V = 64
LAST_V = 64


def tile_mix_save_relu2_bias_kernel(tc, x, w, sm, v4_words, v4_scales, b, out_0, out_1, out_2, out_3):
    nc = tc.nc
    with ExitStack() as ctx:
        keep = ctx.enter_context(tc.tile_pool(name="keep", bufs=1))
        wide = ctx.enter_context(tc.tile_pool(name="wide", bufs=2))
        narrow = ctx.enter_context(tc.tile_pool(name="narrow", bufs=NARROW_BUFS))
        stage = ctx.enter_context(tc.tile_pool(name="stage", bufs=4))
        psum = ctx.enter_context(tc.psum_pool(name="psum", bufs=8))
        ctx.enter_context(tc.manual_schedule())

        codes, scales = {}, {}
        for kind in ("w", "x"):
            for blk in range(NB):
                for g in range(NB):
                    key = (kind, blk, g)
                    codes[key] = keep.tile([P, BLK], U32, name="c%s%d%d" % key, align_bytes=256)
                    scales[key] = keep.tile([P, BLK], U8, name="s%s%d%d" % key, align_bytes=256)
        spans = ((0, 2), (2, 3))
        code_tile, scale_tile, h_codes, h_scales = {}, {}, {}, {}
        for t0, t1 in spans:
            scale_tile[t1 - 1] = keep.tile([P, NB, (t1 - t0) * BLK], U8, name="hs%d" % t0, align_bytes=256)
            for a in range(NB):
                code_tile[(a, t1 - 1)] = keep.tile([P, (t1 - t0) * BLK], U32, name="hc%d%d" % (a, t0), align_bytes=256)
                for tb in range(t0, t1):
                    cols = slice((tb - t0) * BLK, (tb - t0 + 1) * BLK)
                    h_codes[(a, tb)] = code_tile[(a, t1 - 1)][:, cols]
                    h_scales[(a, tb)] = scale_tile[t1 - 1][:, a, cols]
        span_cols = {t1 - 1: slice(t0 * BLK, t1 * BLK) for t0, t1 in spans}
        v_words = keep.tile([P, NB, 2 * N], U8, align_bytes=256)
        v_scales = keep.tile([P, NB, N], U8, align_bytes=256)
        sm_rows = keep.tile([P, BLK], F32, align_bytes=256)
        b_rows = keep.tile([P, P], F32, align_bytes=256)
        ident = keep.tile([P, P], F32, align_bytes=256)
        sm_sb = keep.tile([P, PACK, NB], F32)
        b_sb = keep.tile([P, NT], F32)

        raw, grouped, acc, issued, res_tile, res_view = {}, {}, {}, {}, {}, {}
        done = set()
        order = [(0, 0), (0, 1), (1, 0), (1, 1), (2, 0), (2, 1), (0, 2), (1, 2), ("y", 0), (2, 2), ("y", 1), ("y", 2)]

        def load(kind, b0, b1, g):
            src = (w if kind == "w" else x)[g * BLK : (g + 1) * BLK, b0 * BLK : b1 * BLK]
            if b1 - b0 == 2:
                tl = wide.tile([P, PACK, 2 * BLK], F32, name="wide", align_bytes=256)
            else:
                tl = narrow.tile([P, PACK, BLK], F32, name="narrow", align_bytes=256)
            nc.sync.dma_start(out=tl[:], in_=src.rearrange("(p j) c -> p j c", j=PACK))
            for blk in range(b0, b1):
                raw[(kind, blk, g)] = tl[:, :, (blk - b0) * BLK : (blk - b0 + 1) * BLK]

        def result_tile(unit):
            row, tb = unit
            if row in JOINED and tb == 0:
                tl = wide.tile([P, PACK, 2 * BLK], F32, name="wide", align_bytes=256)
                res_tile[(row, 1)] = (tl, slice(0, 2 * BLK))
                res_view[(row, 0)] = tl[:, :, 0:BLK]
                res_view[(row, 1)] = tl[:, :, BLK : 2 * BLK]
            elif unit not in res_view:
                tl = narrow.tile([P, PACK, BLK], F32, name="narrow", align_bytes=256)
                res_tile[unit] = (tl, slice(tb * BLK, (tb + 1) * BLK))
                res_view[unit] = tl[:]

        def copy_on(engine, out, in_):
            if engine == "v":
                nc.vector.tensor_copy(out=out, in_=in_)
            else:
                nc.scalar.copy(out=out, in_=in_)

        def new_grouped(key):
            grouped[key] = stage.tile([P, PACK * BLK], BF16, name="grouped", align_bytes=256)

        def interleave(engine, key, src, c0, c1):
            copy_on(
                engine,
                grouped[key][:].rearrange("p (c i j) -> p c j i", i=4, j=PACK)[:, c0:c1],
                src.rearrange("p j (c i) -> p c j i", i=4)[:, c0:c1],
            )

        def round_chunk(engine, key):
            new_grouped(key)
            if key[0] == "x":
                interleave(engine, key, raw[key], 0, BLK // 4)
            else:
                copy_on(
                    engine,
                    grouped[key][:].rearrange("p (t m j) -> p m j t", t=PACK, j=PACK),
                    raw[key].rearrange("p j (m t) -> p m j t", t=PACK),
                )

        def quantise_chunk(key):
            nc.vector.quantize_mx(out=codes[key][:].bitcast(FP8X4), scales=scales[key][:], in_=grouped[key][:])
            done.add(key)

        def round_h(engine, unit, c0, c1):
            interleave(engine, unit, res_view[unit], c0, c1)

        def quantise_h(unit):
            a, tb = unit
            nc.vector.quantize_mx(out=h_codes[unit].bitcast(FP8X4), scales=h_scales[unit], in_=grouped[unit][:])
            done.add(unit)
            if tb in span_cols:
                nc.sync.dma_start(
                    out=out_2[a, :, span_cols[tb], :].rearrange("p t i -> p (t i)").bitcast(I32), in_=code_tile[unit][:].bitcast(I32)
                )
                if a == NB - 1:
                    for q in (0, 2, 1, 3):
                        nc.sync.dma_start(
                            out=out_3[:, 4 * q : 4 * q + 4, span_cols[tb]].rearrange("a r t -> r a t").bitcast(I32),
                            in_=scale_tile[tb][QUAD * q : QUAD * q + 4].bitcast(I32),
                        )

        def open_banks(unit):
            for j in range(PACK):
                acc[(unit, j)] = psum.tile([P, BLK], F32, name="acc")

        def one_pass(unit, j, g):
            row, tb = unit
            if row == "y":
                lhs = v_words[:, g, 2 * P * j : 2 * P * (j + 1)].bitcast(FP4X4)
                lhs_scale = v_scales[:, g, P * j : P * (j + 1)]
                rhs, rhs_scale = h_codes[(g, tb)], h_scales[(g, tb)]
            else:
                lhs = codes[("w", row, g)][:, P * j : P * (j + 1)].bitcast(FP8X4)
                lhs_scale = scales[("w", row, g)][:, P * j : P * (j + 1)]
                rhs, rhs_scale = codes[("x", tb, g)][:], scales[("x", tb, g)][:]
            nc.tensor.matmul_mx(
                out=acc[(unit, j)][:], lhsT=lhs, lhsT_scale=lhs_scale, rhs=rhs.bitcast(FP8X4), rhs_scale=rhs_scale,
                start=(g == 0), stop=(g == NB - 1),
            )

        def has_operands(unit, g):
            row, tb = unit
            if row == "y":
                return (g, tb) in done
            return ("w", row, g) in done and ("x", tb, g) in done

        def issue_passes(upto):
            for unit in order[: upto + 1]:
                g0 = issued.get(unit, 0)
                ready = [g for g in range(g0, NB) if all(has_operands(unit, e) for e in range(g0, g + 1))]
                if g0 == 0 and not ready:
                    return
                if g0 == 0:
                    open_banks(unit)
                for j in range(PACK):
                    for g in ready:
                        one_pass(unit, j, g)
                issued[unit] = g0 + len(ready)

        def take(unit, j):
            row = unit[0]
            if j == 0:
                result_tile(unit)
            dst = res_view[unit][:, j, :]
            if row != "y":
                r = stage.tile([P, BLK], F32, name="relu", align_bytes=256, bufs=RELU_BUFS)
                nc.scalar.activation(out=r[:], in_=acc[(unit, j)][:], func=ACT.Relu)
                nc.vector.scalar_tensor_tensor(out=dst, in0=r[:], scalar=sm_sb[:, j, row : row + 1], in1=r[:], op0=ALU.mult, op1=ALU.mult)
            elif j % 2 == 0:
                nc.scalar.activation(out=dst, in_=acc[(unit, j)][:], func=ACT.Identity, bias=b_sb[:, j : j + 1])
            else:
                nc.vector.tensor_scalar(out=dst, in0=acc[(unit, j)][:], scalar1=b_sb[:, j : j + 1], scalar2=None, op0=ALU.add)

        def store(unit, j0, j1):
            row = unit[0]
            if unit in res_tile:
                tl, cols = res_tile[unit]
                if row == "y":
                    dst = out_0[:, cols].rearrange("(j p) t -> p j t", p=P)
                else:
                    dst = out_1[row * BLK : (row + 1) * BLK, cols].rearrange("(p j) t -> p j t", j=PACK)
                nc.sync.dma_start(out=dst[:, j0:j1, :], in_=tl[:, j0:j1, :])

        nc.vector.memset(sm_rows[:], 0.0)
        nc.vector.memset(b_rows[:], 0.0)
        nc.vector.memset(v_scales[:].bitcast(I32), 0)
        make_identity(nc, ident[:])
        chunks = []
        for g in range(NB):
            chunks.extend([("w", 0, g), ("x", 0, g)])
        later = [("x", 1), ("w", 1), ("w", 2), ("x", 2)]
        for kind, blk in later:
            chunks.extend([(kind, blk, g) for g in range(NB)])

        def load_chunk(n):
            if n < len(chunks):
                kind, blk, g = chunks[n]
                load(kind, blk, blk + 1, g)
            if n == len(chunks) - 1:
                nc.sync.dma_start(out=v_words[:].bitcast(I32), in_=v4_words.rearrange("a p n -> p a n").bitcast(I32))
                for q in (0, 2, 1, 3):
                    nc.sync.dma_start(
                        out=v_scales[QUAD * q : QUAD * q + 4].bitcast(I32),
                        in_=v4_scales[:, 4 * q : 4 * q + 4, :].rearrange("a r n -> r a n").bitcast(I32),
                    )

        def prepare(engine, key):
            round_chunk(engine, key)
            load_chunk(chunks.index(key) + NARROW_BUFS)

        load_chunk(0)
        nc.sync.dma_start(out=sm_rows[0:NB, :], in_=sm.rearrange("(a c) -> a c", a=NB))
        nc.sync.dma_start(out=b_rows[0:NT, :], in_=b.rearrange("(n p) -> n p", p=P))
        for n in range(1, NARROW_BUFS):
            load_chunk(n)

        sm_t = psum.tile([P, PACK, P], F32, name="acc")
        b_t = psum.tile([P, P], F32, name="acc")
        for j in range(PACK):
            nc.tensor.transpose(sm_t[:, j, :], sm_rows[:, j:BLK:PACK], ident[:])
        nc.tensor.transpose(b_t[:], b_rows[:], ident[:])

        for g in range(NB):
            prepare("s", ("w", 0, g))
            prepare("v", ("x", 0, g))
            quantise_chunk(("w", 0, g))
            quantise_chunk(("x", 0, g))
            issue_passes(0)
            if g == 1:
                nc.vector.tensor_copy(out=sm_sb[:], in_=sm_t[:, :, 0:NB])
                nc.vector.tensor_copy(out=b_sb[:], in_=b_t[:, 0:NT])

        half = BLK // 8
        rounded = set()
        for cyc, drain in enumerate(order):
            waiting = [u for u in order[:cyc] if u[0] != "y" and u not in done]
            if cyc < len(later):
                keys = [later[cyc] + (g,) for g in range(NB)]
                prepare("v", keys[0])
                for u in waiting:
                    quantise_h(u)
                take(drain, 0)
                quantise_chunk(keys[0])
                issue_passes(cyc + 1)
                for j in range(1, PACK):
                    take(drain, j)
                prepare("s", keys[1])
                if cyc < WHOLE:
                    new_grouped(drain)
                    round_h("s", drain, 0, 2 * half)
                    rounded.add(drain)
                prepare("v", keys[2])
                quantise_chunk(keys[1])
                quantise_chunk(keys[2])
                store(drain, 0, PACK)
            elif cyc < len(order) - 1:
                to_round = [u for u in waiting if u not in rounded]
                share = LAST_V if to_round == [(NB - 1, NB - 1)] else LATE_V
                for u in to_round:
                    new_grouped(u)
                take(drain, 0)
                for u in to_round:
                    round_h("v", u, 0, share)
                take(drain, 1)
                for u in to_round:
                    round_h("s", u, share, 2 * half)
                for u in waiting:
                    quantise_h(u)
                take(drain, 2)
                take(drain, 3)
                store(drain, 0, PACK)
            else:
                for u in waiting:
                    new_grouped(u)
                    round_h("v", u, 0, LAST_V)
                    round_h("s", u, LAST_V, 2 * half)
                    quantise_h(u)
                issue_passes(cyc)
                for j in range(PACK):
                    take(drain, j)
                    if j % 2 == 1:
                        store(drain, j - 1, j + 1)
            issue_passes(cyc + 2)
